import numpy as np
import ml_dtypes


def mxq(x, axis, fmt="e4m3"):
    dtype, down = {"e4m3": (ml_dtypes.float8_e4m3fn, 7), "e5m2": (ml_dtypes.float8_e5m2, 14)}[fmt]
    v = np.moveaxis(np.asarray(x, np.float32).astype(ml_dtypes.bfloat16).astype(np.float64), axis, -1)
    blocks = v.reshape(v.shape[:-1] + (-1, 32))
    amax = np.abs(blocks).max(-1, keepdims=True)
    byte = np.maximum(np.where(amax > 0, np.frexp(amax)[1] - 1 + 127, 0) - down, 1)
    scale = np.exp2(byte - 127.0)
    codes = (blocks / scale).astype(np.float32).astype(dtype).astype(np.float64)
    return np.moveaxis((codes * scale).reshape(v.shape), -1, axis)


WIDE = False


def mx_kscale(k):
    if not WIDE:
        return np.ones(k)
    levels = np.array([30, -30])
    if k % 512:
        return np.exp2(np.random.permutation(np.resize(levels, k // 32))).repeat(32)
    a = np.empty((k // 512, 16))
    for p in range(k // 512):
        a[p, :8] = np.random.permutation(np.resize(levels, 8))
        for g in range(8):
            far = levels[np.abs(levels - a[p, g]) >= 10]
            a[p, g + 8] = far[np.random.randint(len(far))]
    return np.exp2(a.ravel()).repeat(32)


def f64(x):
    return np.asarray(x).astype(np.float64)


def striped(idx):
    return np.tile(np.asarray(idx).reshape(-1, 16).T, (8, 1)).astype(np.uint16)


def unstriped(offs):
    return offs[:16].T.reshape(-1).astype(np.int64)


E2M1 = np.array([0.0, 0.5, 1.0, 1.5, 2.0, 3.0, 4.0, 6.0, -0.0, -0.5, -1.0, -1.5, -2.0, -3.0, -4.0, -6.0])


def pack_weight(w, fmt):
    k, n = w.shape
    w = f64(np.asarray(w, np.float32).astype(ml_dtypes.bfloat16)).reshape(k // 32, 32, n)
    amax = np.abs(w).max(1)
    if fmt in ("e4m3", "e5m2"):
        byte = np.frexp(amax)[1] - 1 + 127 - (7 if fmt == "e4m3" else 14)
    else:
        mant, ex = np.frexp(amax / 6.0)
        byte = np.where(mant > 0.5, ex, ex - 1) + 127
    byte = np.clip(np.where(amax > 0, byte, 1), 1, 254)
    scaled = (w * np.exp2(127.0 - byte)[:, None, :]).reshape(k, n).astype(np.float32)
    by_word = np.ascontiguousarray(scaled.reshape(k // 512, 128, 4, n).transpose(0, 1, 3, 2))
    if fmt in ("e4m3", "e5m2"):
        words = by_word.astype(ml_dtypes.float8_e4m3fn if fmt == "e4m3" else ml_dtypes.float8_e5m2).view(np.uint8)
    else:
        c = by_word.astype(ml_dtypes.float4_e2m1fn).view(np.uint8) & 0xF
        words = (c[..., 0::2] | (c[..., 1::2] << 4)).reshape(k // 512, 128, 2 * n)
    return np.ascontiguousarray(words), np.ascontiguousarray(byte.astype(np.uint8).reshape(k // 512, 16, n))


def unpack_weight(words, scales, fmt):
    g, _, n = scales.shape
    words = np.ascontiguousarray(words).reshape(g, 128, n, -1)
    if fmt in ("e4m3", "e5m2"):
        vals = words.view(ml_dtypes.float8_e4m3fn if fmt == "e4m3" else ml_dtypes.float8_e5m2).astype(np.float64)
    else:
        nib = np.empty((g, 128, n, 4), np.uint8)
        nib[..., 0::2] = words & 0xF
        nib[..., 1::2] = words >> 4
        vals = E2M1[nib]
    vals = vals * np.repeat(np.exp2(scales.astype(np.float64) - 127.0), 8, axis=1)[..., None]
    return vals.transpose(0, 1, 3, 2).reshape(g * 512, n)


K, T, J, R, N = 1024, 1024, 384, 512, 256


def setup_inputs():
    n = np.random.standard_normal
    idx = np.random.permutation(T)[:J]
    fk = mx_kscale(K)
    fr = mx_kscale(R)
    wp = pack_weight(n((K, R)) * 1 / np.sqrt(K) * fk[:, None] * fr, "e5m2")
    wbp = pack_weight(n((R, N)) * 1 / np.sqrt(R) / fr[:, None], "e5m2")
    return {
        "xf": (n((K, T))).astype(np.float32),
        "ow": (n((K, J)) * 0.7).astype(np.float32),
        "fk": (np.random.uniform(0.5, 2.0, (K, 1)) / fk[:, None]).astype(np.float32),
        "w_words": wp[0],
        "w_scales": wp[1],
        "wb_words": wbp[0],
        "wb_scales": wbp[1],
        "rs": (1.0 * n((J, N))).astype(np.float32),
        "offs": striped(idx),
    }


def reference(xf, ow, fk, w_words, w_scales, wb_words, wb_scales, rs, offs):
    idx = unstriped(offs)
    wu = unpack_weight(w_words, w_scales, "e5m2")
    wbu = unpack_weight(wb_words, wb_scales, "e5m2")
    u = (f64(xf)[:, idx] - f64(ow)) * f64(fk)
    uq = mxq(u, 0, "e4m3")
    a = wu.T @ uq
    hid = np.maximum(a, 0.0)
    hidq = mxq(hid, 0, "e4m3")
    p = hidq.T @ wbu
    pk2 = np.max(np.abs(p), axis=1, keepdims=True)
    y = p / (pk2 + 0.2) + 0.3 * f64(rs)
    return y

@@ -1,0 +1,194 @@
+from contextlib import ExitStack
+
+import concourse.mybir as mybir
+
+K, T, J, R, N = 1024, 1024, 384, 512, 256
+FLOPS = 2 * K * R * J + 2 * R * J * N
+
+F32 = mybir.dt.float32
+BF16 = mybir.dt.bfloat16
+I32 = mybir.dt.int32
+U32 = mybir.dt.uint32
+U16 = mybir.dt.uint16
+U8 = mybir.dt.uint8
+E4M3X4 = mybir.dt.float8_e4m3fn_x4
+E5M2X4 = mybir.dt.float8_e5m2_x4
+ALU = mybir.AluOpType
+ACT = mybir.ActivationFunctionType
+
+P = 128
+PACK = 4
+PASSES = K // (P * PACK)
+CHUNK = 128
+CHUNKS = J // CHUNK
+LIST_COLS = CHUNK // 16
+
+
+def tile_list_offsetpicks_plain_rowpeaks_kernel(tc, xf, ow, fk, w_words, w_scales, wb_words, wb_scales, rs, offs, out):
+    nc = tc.nc
+    with ExitStack() as ctx:
+        keep = ctx.enter_context(tc.tile_pool(name="keep", bufs=1))
+        psum = ctx.enter_context(tc.psum_pool(name="psum", bufs=1))
+
+        offsets = keep.tile([P, J // 16], U16, name="offsets")
+        nc.sync.dma_start(offsets[:], offs)
+
+        factors = keep.tile([P, PASSES, PACK], F32, name="factors")
+        nc.scalar.dma_start(factors[:], fk.rearrange("(z p t) o -> p z (t o)", z=PASSES, t=PACK))
+
+        w_scale_rows = keep.tile([P, PASSES, R], U8, name="w_scale_rows", align_bytes=64)
+        wb_scale = keep.tile([P, N], U8, name="wb_scale", align_bytes=64)
+        nc.vector.memset(w_scale_rows[:].bitcast(I32), 0)
+        nc.vector.memset(wb_scale[:].bitcast(I32), 0)
+        for q in range(4):
+            nc.scalar.dma_start(
+                w_scale_rows[32 * q : 32 * q + 4].bitcast(I32),
+                w_scales[:, 4 * q : 4 * q + 4, :].bitcast(I32).rearrange("z r c -> r z c"),
+            )
+        for q in range(4):
+            nc.gpsimd.dma_start(
+                wb_scale[32 * q : 32 * q + 4].bitcast(I32),
+                wb_scales[0, 4 * q : 4 * q + 4, :].bitcast(I32),
+            )
+
+        x_rows = xf.rearrange("(z p t) c -> z t p c", z=PASSES, t=PACK)
+        ow_rows = ow.rearrange("(z p h e) j -> z h p e j", z=PASSES, h=2, e=2)
+        tokens = {}
+        centres = {}
+        w_loaded = {}
+
+        def load_tokens(z, t):
+            tokens[z, t] = keep.tile([P, T], F32, name="tokens_%d_%d" % (z, t))
+            nc.sync.dma_start(tokens[z, t][:], x_rows[z, t])
+
+        def load_centres(z, h):
+            centres[z, h] = keep.tile([P, 2, J], F32, name="centres_%d_%d" % (z, h))
+            nc.sync.dma_start(centres[z, h][:], ow_rows[z, h])
+
+        def load_w(z):
+            w_loaded[z] = keep.tile([P, R], U32, name="w_loaded_%d" % z)
+            nc.sync.dma_start(w_loaded[z][:].bitcast(I32), w_words[z].rearrange("p c t -> p (c t)").bitcast(I32))
+
+        load_centres(0, 0)
+        load_tokens(0, 0)
+        load_tokens(0, 1)
+        load_w(0)
+        load_centres(0, 1)
+        load_tokens(0, 2)
+        load_w(1)
+        load_centres(1, 0)
+        load_tokens(1, 0)
+        load_tokens(1, 1)
+        load_tokens(0, 3)
+        load_centres(1, 1)
+        load_tokens(1, 2)
+        load_tokens(1, 3)
+        wb_codes = keep.tile([P, N], U32, name="wb_codes", align_bytes=64)
+        nc.sync.dma_start(wb_codes[:].bitcast(I32), wb_words[0].rearrange("p c t -> p (c t)").bitcast(I32))
+        residual = keep.tile([P, CHUNKS, N], F32, name="residual")
+        nc.sync.dma_start(residual[:], rs.rearrange("(c p) n -> p c n", p=P))
+
+        u_bf16 = {}
+        for z in range(PASSES):
+            for c in range(CHUNKS):
+                u_bf16[z, c] = keep.tile([P, CHUNK, PACK], BF16, name="u_bf16_%d_%d" % (z, c), align_bytes=64)
+
+        def make_u(z, t):
+            for c in range(CHUNKS):
+                diff = keep.tile([P, CHUNK], F32, name="diff_%d_%d_%d" % (z, t, c))
+                picked = tokens[z, t][:].indirect(offsets[:, c * LIST_COLS : (c + 1) * LIST_COLS])
+                centre = centres[z, t // 2][:, t % 2, c * CHUNK : (c + 1) * CHUNK]
+                nc.vector.tensor_tensor(diff[:], picked, centre, ALU.subtract)
+                nc.scalar.activation(u_bf16[z, c][:, :, t], diff[:], ACT.Copy, scale=factors[:, z, t : t + 1])
+
+        def quantize(source, name):
+            codes = keep.tile([P, CHUNK], U32, name=name + "_codes", align_bytes=64)
+            scales = keep.tile([P, CHUNK], U8, name=name + "_scales", align_bytes=64)
+            nc.vector.quantize_mx(out=codes[:].bitcast(E4M3X4), scales=scales[:], in_=source[:].rearrange("p j t -> p (j t)"))
+            return codes, scales
+
+        w_codes = {}
+
+        def deal_w(z):
+            w_codes[z] = keep.tile([P, PACK, P], U32, name="w_codes_%d" % z, align_bytes=64)
+            nc.vector.tensor_copy(
+                w_codes[z][:].rearrange("p t (b i) -> p b t i", i=4),
+                w_loaded[z][:].rearrange("p (b i t) -> p b t i", i=4, t=PACK),
+            )
+
+        w_scale = keep.tile([P, PACK, PASSES, P], U8, name="w_scale", align_bytes=64)
+
+        def deal_w_scales():
+            nc.vector.tensor_copy(
+                w_scale[:].rearrange("p t z (b i) -> p (z b) t i", i=16),
+                w_scale_rows[:].rearrange("p z (b i t) -> p (z b) t i", i=16, t=PACK),
+            )
+
+        a_psum = [psum.tile([P, PACK, CHUNK], F32, name="a_psum_%d" % c) for c in range(CHUNKS)]
+        p_psum = [psum.tile([P, N], F32, name="p_psum_%d" % c) for c in range(CHUNKS)]
+
+        def first_product(z, c):
+            codes, scales = quantize(u_bf16[z, c], "u_%d_%d" % (z, c))
+            for t in range(PACK):
+                nc.tensor.matmul_mx(
+                    out=a_psum[c][:, t, :],
+                    lhsT=w_codes[z][:, t, :].bitcast(E5M2X4),
+                    lhsT_scale=w_scale[:, t, z, :],
+                    rhs=codes[:].bitcast(E4M3X4),
+                    rhs_scale=scales[:],
+                    start=(z == 0 and t == 0),
+                    stop=(z == PASSES - 1 and t == PACK - 1),
+                )
+
+        make_u(0, 0)
+        make_u(0, 1)
+        deal_w(0)
+        make_u(0, 2)
+        deal_w(1)
+        deal_w_scales()
+        make_u(1, 0)
+        make_u(1, 1)
+        make_u(0, 3)
+        for c in range(CHUNKS):
+            first_product(0, c)
+        make_u(1, 2)
+        make_u(1, 3)
+        for c in range(CHUNKS):
+            first_product(1, c)
+
+        hid = [keep.tile([P, CHUNK, PACK], BF16, name="hid_%d" % c, align_bytes=64) for c in range(CHUNKS)]
+        for c in range(CHUNKS):
+            sums = a_psum[c][:].rearrange("p t j -> p j t")
+            if c == 1:
+                nc.vector.tensor_scalar_max(hid[c][:], sums, 0.0)
+            else:
+                nc.scalar.activation(hid[c][:], sums, ACT.Relu)
+
+        for c in range(CHUNKS):
+            codes, scales = quantize(hid[c], "hid_%d" % c)
+            nc.tensor.matmul_mx(
+                out=p_psum[c][:],
+                lhsT=codes[:].bitcast(E4M3X4),
+                lhsT_scale=scales[:],
+                rhs=wb_codes[:].bitcast(E5M2X4),
+                rhs_scale=wb_scale[:],
+                start=True,
+                stop=True,
+            )
+
+        scaled_residual = [keep.tile([P, N], F32, name="scaled_residual_%d" % c) for c in range(CHUNKS)]
+        for c in range(CHUNKS):
+            nc.vector.tensor_scalar_mul(scaled_residual[c][:], residual[:, c, :], 0.3)
+
+        inverse = []
+        for c in range(CHUNKS):
+            size = keep.tile([P, N], F32, name="size_%d" % c)
+            nc.scalar.activation(size[:], p_psum[c][:], ACT.Abs)
+            divisor = keep.tile([P, 1], F32, name="divisor_%d" % c)
+            nc.vector.tensor_scalar(size[:], size[:], 0.2, None, ALU.add, ALU.max, accum_out=divisor[:])
+            inverse.append(keep.tile([P, 1], F32, name="inverse_%d" % c))
+            nc.vector.reciprocal(inverse[c][:], divisor[:])
+        for c in range(CHUNKS):
+            result = keep.tile([P, N], F32, name="result_%d" % c)
+            nc.vector.scalar_tensor_tensor(result[:], p_psum[c][:], inverse[c][:], scaled_residual[c][:], ALU.mult, ALU.add)
+            nc.sync.dma_start(out[c * CHUNK : (c + 1) * CHUNK, :], result[:])

@@ -41,7 +41,7 @@ def tile_list_offsetpicks_plain_rowpeaks_kernel(tc, xf, ow, fk, w_words, w_scale
         nc.vector.memset(w_scale_rows[:].bitcast(I32), 0)
         nc.vector.memset(wb_scale[:].bitcast(I32), 0)
         for q in range(4):
-            nc.scalar.dma_start(
+            nc.gpsimd.dma_start(
                 w_scale_rows[32 * q : 32 * q + 4].bitcast(I32),
                 w_scales[:, 4 * q : 4 * q + 4, :].bitcast(I32).rearrange("z r c -> r z c"),
             )
@@ -52,7 +52,7 @@ def tile_list_offsetpicks_plain_rowpeaks_kernel(tc, xf, ow, fk, w_words, w_scale
             )
 
         x_rows = xf.rearrange("(z p t) c -> z t p c", z=PASSES, t=PACK)
-        ow_rows = ow.rearrange("(z p h e) j -> z h p e j", z=PASSES, h=2, e=2)
+        ow_rows = ow.rearrange("(z p t) j -> z p t j", z=PASSES, t=PACK)
         tokens = {}
         centres = {}
         w_loaded = {}
@@ -61,26 +61,27 @@ def tile_list_offsetpicks_plain_rowpeaks_kernel(tc, xf, ow, fk, w_words, w_scale
             tokens[z, t] = keep.tile([P, T], F32, name="tokens_%d_%d" % (z, t))
             nc.sync.dma_start(tokens[z, t][:], x_rows[z, t])
 
-        def load_centres(z, h):
-            centres[z, h] = keep.tile([P, 2, J], F32, name="centres_%d_%d" % (z, h))
-            nc.sync.dma_start(centres[z, h][:], ow_rows[z, h])
+        def load_centres(z, first, count):
+            rows = keep.tile([P, count, J], F32, name="centres_%d_%d" % (z, first))
+            nc.sync.dma_start(rows[:], ow_rows[z, :, first : first + count, :])
+            for t in range(count):
+                centres[z, first + t] = rows[:, t, :]
 
         def load_w(z):
             w_loaded[z] = keep.tile([P, R], U32, name="w_loaded_%d" % z)
             nc.sync.dma_start(w_loaded[z][:].bitcast(I32), w_words[z].rearrange("p c t -> p (c t)").bitcast(I32))
 
-        load_centres(0, 0)
+        load_centres(0, 0, 4)
         load_tokens(0, 0)
         load_tokens(0, 1)
-        load_w(0)
-        load_centres(0, 1)
         load_tokens(0, 2)
+        load_tokens(0, 3)
         load_w(1)
-        load_centres(1, 0)
+        load_centres(1, 0, 2)
         load_tokens(1, 0)
         load_tokens(1, 1)
-        load_tokens(0, 3)
-        load_centres(1, 1)
+        load_centres(1, 2, 2)
+        load_w(0)
         load_tokens(1, 2)
         load_tokens(1, 3)
         wb_codes = keep.tile([P, N], U32, name="wb_codes", align_bytes=64)
@@ -95,9 +96,9 @@ def tile_list_offsetpicks_plain_rowpeaks_kernel(tc, xf, ow, fk, w_words, w_scale
 
         def make_u(z, t):
             for c in range(CHUNKS):
-                diff = keep.tile([P, CHUNK], F32, name="diff_%d_%d_%d" % (z, t, c))
+                diff = keep.tile([P, CHUNK], F32, name="diff_%d_%d_%d" % (z, t, c), align_bytes=64)
                 picked = tokens[z, t][:].indirect(offsets[:, c * LIST_COLS : (c + 1) * LIST_COLS])
-                centre = centres[z, t // 2][:, t % 2, c * CHUNK : (c + 1) * CHUNK]
+                centre = centres[z, t][:, c * CHUNK : (c + 1) * CHUNK]
                 nc.vector.tensor_tensor(diff[:], picked, centre, ALU.subtract)
                 nc.scalar.activation(u_bf16[z, c][:, :, t], diff[:], ACT.Copy, scale=factors[:, z, t : t + 1])
 
@@ -111,24 +112,23 @@ def tile_list_offsetpicks_plain_rowpeaks_kernel(tc, xf, ow, fk, w_words, w_scale
 
         def deal_w(z):
             w_codes[z] = keep.tile([P, PACK, P], U32, name="w_codes_%d" % z, align_bytes=64)
-            nc.vector.tensor_copy(
+            nc.scalar.copy(
                 w_codes[z][:].rearrange("p t (b i) -> p b t i", i=4),
                 w_loaded[z][:].rearrange("p (b i t) -> p b t i", i=4, t=PACK),
             )
 
-        w_scale = keep.tile([P, PACK, PASSES, P], U8, name="w_scale", align_bytes=64)
-
         def deal_w_scales():
+            dealt = keep.tile([P, PACK, PASSES, P], U8, name="w_scale", tag="diff_0_3_2", align_bytes=64)
             nc.vector.tensor_copy(
-                w_scale[:].rearrange("p t z (b i) -> p (z b) t i", i=16),
+                dealt[:].rearrange("p t z (b i) -> p (z b) t i", i=16),
                 w_scale_rows[:].rearrange("p z (b i t) -> p (z b) t i", i=16, t=PACK),
             )
+            return dealt
 
         a_psum = [psum.tile([P, PACK, CHUNK], F32, name="a_psum_%d" % c) for c in range(CHUNKS)]
         p_psum = [psum.tile([P, N], F32, name="p_psum_%d" % c) for c in range(CHUNKS)]
 
-        def first_product(z, c):
-            codes, scales = quantize(u_bf16[z, c], "u_%d_%d" % (z, c))
+        def first_product(z, c, codes, scales):
             for t in range(PACK):
                 nc.tensor.matmul_mx(
                     out=a_psum[c][:, t, :],
@@ -140,21 +140,20 @@ def tile_list_offsetpicks_plain_rowpeaks_kernel(tc, xf, ow, fk, w_words, w_scale
                     stop=(z == PASSES - 1 and t == PACK - 1),
                 )
 
-        make_u(0, 0)
-        make_u(0, 1)
-        deal_w(0)
-        make_u(0, 2)
+        for t in range(PACK):
+            make_u(0, t)
         deal_w(1)
-        deal_w_scales()
+        u_first = [quantize(u_bf16[0, c], "u_0_%d" % c) for c in range(CHUNKS)]
+        w_scale = deal_w_scales()
         make_u(1, 0)
         make_u(1, 1)
-        make_u(0, 3)
+        deal_w(0)
         for c in range(CHUNKS):
-            first_product(0, c)
+            first_product(0, c, *u_first[c])
         make_u(1, 2)
         make_u(1, 3)
         for c in range(CHUNKS):
-            first_product(1, c)
+            first_product(1, c, *quantize(u_bf16[1, c], "u_1_%d" % c))
 
         hid = [keep.tile([P, CHUNK, PACK], BF16, name="hid_%d" % c, align_bytes=64) for c in range(CHUNKS)]
         for c in range(CHUNKS):

@@ -41,16 +41,10 @@ def tile_list_offsetpicks_plain_rowpeaks_kernel(tc, xf, ow, fk, w_words, w_scale
         nc.vector.memset(w_scale_rows[:].bitcast(I32), 0)
         nc.vector.memset(wb_scale[:].bitcast(I32), 0)
         for q in range(4):
-            nc.gpsimd.dma_start(
+            nc.scalar.dma_start(
                 w_scale_rows[32 * q : 32 * q + 4].bitcast(I32),
                 w_scales[:, 4 * q : 4 * q + 4, :].bitcast(I32).rearrange("z r c -> r z c"),
             )
-        for q in range(4):
-            nc.gpsimd.dma_start(
-                wb_scale[32 * q : 32 * q + 4].bitcast(I32),
-                wb_scales[0, 4 * q : 4 * q + 4, :].bitcast(I32),
-            )
-
         x_rows = xf.rearrange("(z p t) c -> z t p c", z=PASSES, t=PACK)
         ow_rows = ow.rearrange("(z p t) j -> z p t j", z=PASSES, t=PACK)
         tokens = {}
@@ -89,36 +83,47 @@ def tile_list_offsetpicks_plain_rowpeaks_kernel(tc, xf, ow, fk, w_words, w_scale
         residual = keep.tile([P, CHUNKS, N], F32, name="residual")
         nc.sync.dma_start(residual[:], rs.rearrange("(c p) n -> p c n", p=P))
 
-        u_bf16 = {}
-        for z in range(PASSES):
-            for c in range(CHUNKS):
-                u_bf16[z, c] = keep.tile([P, CHUNK, PACK], BF16, name="u_bf16_%d_%d" % (z, c), align_bytes=64)
+        for q in range(4):
+            nc.sync.dma_start(
+                wb_scale[32 * q : 32 * q + 4].bitcast(I32),
+                wb_scales[0, 4 * q : 4 * q + 4, :].bitcast(I32),
+            )
 
-        def make_u(z, t):
-            for c in range(CHUNKS):
-                diff = keep.tile([P, CHUNK], F32, name="diff_%d_%d_%d" % (z, t, c), align_bytes=64)
-                picked = tokens[z, t][:].indirect(offsets[:, c * LIST_COLS : (c + 1) * LIST_COLS])
-                centre = centres[z, t][:, c * CHUNK : (c + 1) * CHUNK]
-                nc.vector.tensor_tensor(diff[:], picked, centre, ALU.subtract)
-                nc.scalar.activation(u_bf16[z, c][:, :, t], diff[:], ACT.Copy, scale=factors[:, z, t : t + 1])
+        u_rows = [
+            keep.tile([P, CHUNKS, PACK, CHUNK], BF16, name=name, align_bytes=64) for name in ("early_rows", "late_rows")
+        ]
+
+        def make_u_rows(z, t, first, count, differences):
+            width = count * CHUNK
+            diff = differences[:, first * CHUNK : first * CHUNK + width]
+            picked = tokens[z, t][:].indirect(offsets[:, first * LIST_COLS : (first + count) * LIST_COLS])
+            centre = centres[z, t][:, first * CHUNK : first * CHUNK + width]
+            nc.vector.tensor_tensor(diff, picked, centre, ALU.subtract)
+            nc.scalar.activation(
+                u_rows[z][:, first : first + count, t, :],
+                diff.rearrange("p (c j) -> p c j", j=CHUNK),
+                ACT.Copy,
+                scale=factors[:, z, t : t + 1],
+            )
 
         def quantize(source, name):
-            codes = keep.tile([P, CHUNK], U32, name=name + "_codes", align_bytes=64)
-            scales = keep.tile([P, CHUNK], U8, name=name + "_scales", align_bytes=64)
+            width = source.shape[1]
+            codes = keep.tile([P, width], U32, name=name + "_codes", align_bytes=64)
+            scales = keep.tile([P, width], U8, name=name + "_scales", align_bytes=64)
             nc.vector.quantize_mx(out=codes[:].bitcast(E4M3X4), scales=scales[:], in_=source[:].rearrange("p j t -> p (j t)"))
             return codes, scales
 
         w_codes = {}
 
-        def deal_w(z):
-            w_codes[z] = keep.tile([P, PACK, P], U32, name="w_codes_%d" % z, align_bytes=64)
+        def deal_w(z, buffer):
+            w_codes[z] = keep.tile([P, PACK, P], U32, name="w_codes_%d" % z, tag=buffer, align_bytes=64)
             nc.scalar.copy(
                 w_codes[z][:].rearrange("p t (b i) -> p b t i", i=4),
                 w_loaded[z][:].rearrange("p (b i t) -> p b t i", i=4, t=PACK),
             )
 
         def deal_w_scales():
-            dealt = keep.tile([P, PACK, PASSES, P], U8, name="w_scale", tag="diff_0_3_2", align_bytes=64)
+            dealt = keep.tile([P, PACK, PASSES, P], U8, name="w_scale", tag="diff_0_2", align_bytes=64)
             nc.vector.tensor_copy(
                 dealt[:].rearrange("p t z (b i) -> p (z b) t i", i=16),
                 w_scale_rows[:].rearrange("p z (b i t) -> p (z b) t i", i=16, t=PACK),
@@ -134,26 +139,38 @@ def tile_list_offsetpicks_plain_rowpeaks_kernel(tc, xf, ow, fk, w_words, w_scale
                     out=a_psum[c][:, t, :],
                     lhsT=w_codes[z][:, t, :].bitcast(E5M2X4),
                     lhsT_scale=w_scale[:, t, z, :],
-                    rhs=codes[:].bitcast(E4M3X4),
-                    rhs_scale=scales[:],
+                    rhs=codes.bitcast(E4M3X4),
+                    rhs_scale=scales,
                     start=(z == 0 and t == 0),
                     stop=(z == PASSES - 1 and t == PACK - 1),
                 )
 
         for t in range(PACK):
-            make_u(0, t)
-        deal_w(1)
-        u_first = [quantize(u_bf16[0, c], "u_0_%d" % c) for c in range(CHUNKS)]
+            make_u_rows(0, t, 0, CHUNKS, keep.tile([P, J], F32, name="diff_0_%d" % t, align_bytes=64))
+        u_early = keep.tile([P, J, PACK], BF16, name="u_early", align_bytes=64)
+        nc.scalar.copy(u_early[:].rearrange("p (c j) t -> p c j t", j=CHUNK), u_rows[0][:].rearrange("p c t j -> p c j t"))
+        early_codes, early_scales = quantize(u_early, "u_early")
         w_scale = deal_w_scales()
-        make_u(1, 0)
-        make_u(1, 1)
-        deal_w(0)
+        deal_w(1, "diff_0_3")
+        make_u_rows(1, 0, 0, CHUNKS, keep.tile([P, J], F32, name="diff_1_0", align_bytes=64))
+        make_u_rows(1, 1, 0, CHUNKS, keep.tile([P, J], F32, name="diff_1_1", align_bytes=64))
+        deal_w(0, "diff_1_0")
         for c in range(CHUNKS):
-            first_product(0, c, *u_first[c])
-        make_u(1, 2)
-        make_u(1, 3)
+            cols = slice(c * CHUNK, (c + 1) * CHUNK)
+            first_product(0, c, early_codes[:, cols], early_scales[:, cols])
+        late_diff = keep.tile([P, J], F32, name="late_diff", tag="u_early", align_bytes=64)
+        for t in (2, 3):
+            for c in range(CHUNKS):
+                make_u_rows(1, t, c, 1, late_diff)
+        u_late = [keep.tile([P, CHUNK, PACK], BF16, name="u_late_%d" % c, align_bytes=64) for c in range(CHUNKS)]
         for c in range(CHUNKS):
-            first_product(1, c, *quantize(u_bf16[1, c], "u_1_%d" % c))
+            nc.vector.tensor_copy(u_late[c][:], u_rows[1][:, c].rearrange("p t j -> p j t"))
+        for c in range(CHUNKS):
+            codes, scales = quantize(u_late[c], "u_late_%d" % c)
+            first_product(1, c, codes[:], scales[:])
+
+        scaled_residual = keep.tile([P, CHUNKS, N], F32, name="scaled_residual", tag="u_early", align_bytes=64)
+        nc.scalar.activation(scaled_residual[:], residual[:], ACT.Copy, scale=0.3)
 
         hid = [keep.tile([P, CHUNK, PACK], BF16, name="hid_%d" % c, align_bytes=64) for c in range(CHUNKS)]
         for c in range(CHUNKS):
@@ -175,10 +192,6 @@ def tile_list_offsetpicks_plain_rowpeaks_kernel(tc, xf, ow, fk, w_words, w_scale
                 stop=True,
             )
 
-        scaled_residual = [keep.tile([P, N], F32, name="scaled_residual_%d" % c) for c in range(CHUNKS)]
-        for c in range(CHUNKS):
-            nc.vector.tensor_scalar_mul(scaled_residual[c][:], residual[:, c, :], 0.3)
-
         inverse = []
         for c in range(CHUNKS):
             size = keep.tile([P, N], F32, name="size_%d" % c)
@@ -189,5 +202,5 @@ def tile_list_offsetpicks_plain_rowpeaks_kernel(tc, xf, ow, fk, w_words, w_scale
             nc.vector.reciprocal(inverse[c][:], divisor[:])
         for c in range(CHUNKS):
             result = keep.tile([P, N], F32, name="result_%d" % c)
-            nc.vector.scalar_tensor_tensor(result[:], p_psum[c][:], inverse[c][:], scaled_residual[c][:], ALU.mult, ALU.add)
+            nc.vector.scalar_tensor_tensor(result[:], p_psum[c][:], inverse[c][:], scaled_residual[:, c, :], ALU.mult, ALU.add)
             nc.sync.dma_start(out[c * CHUNK : (c + 1) * CHUNK, :], result[:])

@@ -34,14 +34,14 @@ def tile_list_offsetpicks_plain_rowpeaks_kernel(tc, xf, ow, fk, w_words, w_scale
         nc.sync.dma_start(offsets[:], offs)
 
         factors = keep.tile([P, PASSES, PACK], F32, name="factors")
-        nc.scalar.dma_start(factors[:], fk.rearrange("(z p t) o -> p z (t o)", z=PASSES, t=PACK))
+        nc.sync.dma_start(factors[:], fk.rearrange("(z p t) o -> p z (t o)", z=PASSES, t=PACK))
 
         w_scale_rows = keep.tile([P, PASSES, R], U8, name="w_scale_rows", align_bytes=64)
         wb_scale = keep.tile([P, N], U8, name="wb_scale", align_bytes=64)
-        nc.vector.memset(w_scale_rows[:].bitcast(I32), 0)
-        nc.vector.memset(wb_scale[:].bitcast(I32), 0)
+        nc.gpsimd.memset(w_scale_rows[:].bitcast(I32), 0)
+        nc.gpsimd.memset(wb_scale[:].bitcast(I32), 0)
         for q in range(4):
-            nc.scalar.dma_start(
+            nc.gpsimd.dma_start(
                 w_scale_rows[32 * q : 32 * q + 4].bitcast(I32),
                 w_scales[:, 4 * q : 4 * q + 4, :].bitcast(I32).rearrange("z r c -> r z c"),
             )
@@ -65,12 +65,12 @@ def tile_list_offsetpicks_plain_rowpeaks_kernel(tc, xf, ow, fk, w_words, w_scale
             w_loaded[z] = keep.tile([P, R], U32, name="w_loaded_%d" % z)
             nc.sync.dma_start(w_loaded[z][:].bitcast(I32), w_words[z].rearrange("p c t -> p (c t)").bitcast(I32))
 
-        load_centres(0, 0, 4)
+        load_centres(0, 0, 2)
         load_tokens(0, 0)
         load_tokens(0, 1)
+        load_centres(0, 2, 2)
         load_tokens(0, 2)
         load_tokens(0, 3)
-        load_w(1)
         load_centres(1, 0, 2)
         load_tokens(1, 0)
         load_tokens(1, 1)
@@ -78,6 +78,7 @@ def tile_list_offsetpicks_plain_rowpeaks_kernel(tc, xf, ow, fk, w_words, w_scale
         load_w(0)
         load_tokens(1, 2)
         load_tokens(1, 3)
+        load_w(1)
         wb_codes = keep.tile([P, N], U32, name="wb_codes", align_bytes=64)
         nc.sync.dma_start(wb_codes[:].bitcast(I32), wb_words[0].rearrange("p c t -> p (c t)").bitcast(I32))
         residual = keep.tile([P, CHUNKS, N], F32, name="residual")
@@ -148,12 +149,14 @@ def tile_list_offsetpicks_plain_rowpeaks_kernel(tc, xf, ow, fk, w_words, w_scale
         for t in range(PACK):
             make_u_rows(0, t, 0, CHUNKS, keep.tile([P, J], F32, name="diff_0_%d" % t, align_bytes=64))
         u_early = keep.tile([P, J, PACK], BF16, name="u_early", align_bytes=64)
-        nc.scalar.copy(u_early[:].rearrange("p (c j) t -> p c j t", j=CHUNK), u_rows[0][:].rearrange("p c t j -> p c j t"))
+        nc.scalar.copy(
+            u_early[:].rearrange("p (c b i) t -> p c b t i", c=CHUNKS, i=4),
+            u_rows[0][:].rearrange("p c t (b i) -> p c b t i", i=4),
+        )
         early_codes, early_scales = quantize(u_early, "u_early")
         w_scale = deal_w_scales()
-        deal_w(1, "diff_0_3")
         make_u_rows(1, 0, 0, CHUNKS, keep.tile([P, J], F32, name="diff_1_0", align_bytes=64))
-        make_u_rows(1, 1, 0, CHUNKS, keep.tile([P, J], F32, name="diff_1_1", align_bytes=64))
+        make_u_rows(1, 1, 0, CHUNKS, keep.tile([P, J], F32, name="diff_1_1", tag="w_scale_rows", align_bytes=64))
         deal_w(0, "diff_1_0")
         for c in range(CHUNKS):
             cols = slice(c * CHUNK, (c + 1) * CHUNK)
@@ -162,15 +165,16 @@ def tile_list_offsetpicks_plain_rowpeaks_kernel(tc, xf, ow, fk, w_words, w_scale
         for t in (2, 3):
             for c in range(CHUNKS):
                 make_u_rows(1, t, c, 1, late_diff)
+        deal_w(1, "u_early")
         u_late = [keep.tile([P, CHUNK, PACK], BF16, name="u_late_%d" % c, align_bytes=64) for c in range(CHUNKS)]
         for c in range(CHUNKS):
-            nc.vector.tensor_copy(u_late[c][:], u_rows[1][:, c].rearrange("p t j -> p j t"))
+            nc.vector.tensor_copy(
+                u_late[c][:].rearrange("p (b i) t -> p b t i", i=4),
+                u_rows[1][:, c].rearrange("p t (b i) -> p b t i", i=4),
+            )
         for c in range(CHUNKS):
             codes, scales = quantize(u_late[c], "u_late_%d" % c)
             first_product(1, c, codes[:], scales[:])
-
-        scaled_residual = keep.tile([P, CHUNKS, N], F32, name="scaled_residual", tag="u_early", align_bytes=64)
-        nc.scalar.activation(scaled_residual[:], residual[:], ACT.Copy, scale=0.3)
 
         hid = [keep.tile([P, CHUNK, PACK], BF16, name="hid_%d" % c, align_bytes=64) for c in range(CHUNKS)]
         for c in range(CHUNKS):
@@ -179,6 +183,10 @@ def tile_list_offsetpicks_plain_rowpeaks_kernel(tc, xf, ow, fk, w_words, w_scale
                 nc.vector.tensor_scalar_max(hid[c][:], sums, 0.0)
             else:
                 nc.scalar.activation(hid[c][:], sums, ACT.Relu)
+
+        scaled_residual = keep.tile([P, CHUNKS, N], F32, name="scaled_residual", tag="w_loaded_1")
+        for c in range(CHUNKS):
+            nc.scalar.activation(scaled_residual[:, c, :], residual[:, c, :], ACT.Copy, scale=0.3)
 
         for c in range(CHUNKS):
             codes, scales = quantize(hid[c], "hid_%d" % c)

from contextlib import ExitStack

import concourse.mybir as mybir

K, T, J, R, N = 1024, 1024, 384, 512, 256
FLOPS = 2 * K * R * J + 2 * R * J * N

F32 = mybir.dt.float32
BF16 = mybir.dt.bfloat16
I32 = mybir.dt.int32
U32 = mybir.dt.uint32
U16 = mybir.dt.uint16
U8 = mybir.dt.uint8
E4M3X4 = mybir.dt.float8_e4m3fn_x4
E5M2X4 = mybir.dt.float8_e5m2_x4
ALU = mybir.AluOpType
ACT = mybir.ActivationFunctionType

P = 128
PACK = 4
PASSES = K // (P * PACK)
CHUNK = 128
CHUNKS = J // CHUNK
LIST_COLS = CHUNK // 16


def tile_list_offsetpicks_plain_rowpeaks_kernel(tc, xf, ow, fk, w_words, w_scales, wb_words, wb_scales, rs, offs, out):
    nc = tc.nc
    with ExitStack() as ctx:
        keep = ctx.enter_context(tc.tile_pool(name="keep", bufs=1))
        psum = ctx.enter_context(tc.psum_pool(name="psum", bufs=1))

        offsets = keep.tile([P, J // 16], U16, name="offsets")
        nc.sync.dma_start(offsets[:], offs)

        factors = keep.tile([P, PASSES, PACK], F32, name="factors")
        nc.sync.dma_start(factors[:], fk.rearrange("(z p t) o -> p z (t o)", z=PASSES, t=PACK))

        w_scale_rows = keep.tile([P, PASSES, R], U8, name="w_scale_rows", align_bytes=64)
        wb_scale = keep.tile([P, N], U8, name="wb_scale", align_bytes=64)
        nc.gpsimd.memset(w_scale_rows[:].bitcast(I32), 0)
        nc.gpsimd.memset(wb_scale[:].bitcast(I32), 0)
        for q in range(4):
            nc.gpsimd.dma_start(
                w_scale_rows[32 * q : 32 * q + 4].bitcast(I32),
                w_scales[:, 4 * q : 4 * q + 4, :].bitcast(I32).rearrange("z r c -> r z c"),
            )
        x_rows = xf.rearrange("(z p t) c -> z t p c", z=PASSES, t=PACK)
        ow_rows = ow.rearrange("(z p t) j -> z p t j", z=PASSES, t=PACK)
        tokens = {}
        centres = {}
        w_loaded = {}

        def load_tokens(z, t):
            tokens[z, t] = keep.tile([P, T], F32, name="tokens_%d_%d" % (z, t))
            nc.sync.dma_start(tokens[z, t][:], x_rows[z, t])

        def load_centres(z, first, count):
            rows = keep.tile([P, count, J], F32, name="centres_%d_%d" % (z, first))
            nc.sync.dma_start(rows[:], ow_rows[z, :, first : first + count, :])
            for t in range(count):
                centres[z, first + t] = rows[:, t, :]

        def load_w(z):
            w_loaded[z] = keep.tile([P, R], U32, name="w_loaded_%d" % z)
            nc.sync.dma_start(w_loaded[z][:].bitcast(I32), w_words[z].rearrange("p c t -> p (c t)").bitcast(I32))

        load_centres(0, 0, 2)
        load_tokens(0, 0)
        load_tokens(0, 1)
        load_centres(0, 2, 2)
        load_tokens(0, 2)
        load_tokens(0, 3)
        load_centres(1, 0, 2)
        load_tokens(1, 0)
        load_tokens(1, 1)
        load_centres(1, 2, 2)
        load_w(0)
        load_tokens(1, 2)
        load_tokens(1, 3)
        load_w(1)
        wb_codes = keep.tile([P, N], U32, name="wb_codes", align_bytes=64)
        nc.sync.dma_start(wb_codes[:].bitcast(I32), wb_words[0].rearrange("p c t -> p (c t)").bitcast(I32))
        residual = keep.tile([P, CHUNKS, N], F32, name="residual")
        nc.sync.dma_start(residual[:], rs.rearrange("(c p) n -> p c n", p=P))

        for q in range(4):
            nc.sync.dma_start(
                wb_scale[32 * q : 32 * q + 4].bitcast(I32),
                wb_scales[0, 4 * q : 4 * q + 4, :].bitcast(I32),
            )

        u_rows = [
            keep.tile([P, CHUNKS, PACK, CHUNK], BF16, name=name, align_bytes=64) for name in ("early_rows", "late_rows")
        ]

        def make_u_rows(z, t, first, count, differences):
            width = count * CHUNK
            diff = differences[:, first * CHUNK : first * CHUNK + width]
            picked = tokens[z, t][:].indirect(offsets[:, first * LIST_COLS : (first + count) * LIST_COLS])
            centre = centres[z, t][:, first * CHUNK : first * CHUNK + width]
            nc.vector.tensor_tensor(diff, picked, centre, ALU.subtract)
            nc.scalar.activation(
                u_rows[z][:, first : first + count, t, :],
                diff.rearrange("p (c j) -> p c j", j=CHUNK),
                ACT.Copy,
                scale=factors[:, z, t : t + 1],
            )

        def quantize(source, name):
            width = source.shape[1]
            codes = keep.tile([P, width], U32, name=name + "_codes", align_bytes=64)
            scales = keep.tile([P, width], U8, name=name + "_scales", align_bytes=64)
            nc.vector.quantize_mx(out=codes[:].bitcast(E4M3X4), scales=scales[:], in_=source[:].rearrange("p j t -> p (j t)"))
            return codes, scales

        w_codes = {}

        def deal_w(z, buffer):
            w_codes[z] = keep.tile([P, PACK, P], U32, name="w_codes_%d" % z, tag=buffer, align_bytes=64)
            nc.scalar.copy(
                w_codes[z][:].rearrange("p t (b i) -> p b t i", i=4),
                w_loaded[z][:].rearrange("p (b i t) -> p b t i", i=4, t=PACK),
            )

        def deal_w_scales():
            dealt = keep.tile([P, PACK, PASSES, P], U8, name="w_scale", tag="diff_0_2", align_bytes=64)
            nc.vector.tensor_copy(
                dealt[:].rearrange("p t z (b i) -> p (z b) t i", i=16),
                w_scale_rows[:].rearrange("p z (b i t) -> p (z b) t i", i=16, t=PACK),
            )
            return dealt

        a_psum = [psum.tile([P, PACK, CHUNK], F32, name="a_psum_%d" % c) for c in range(CHUNKS)]
        p_psum = [psum.tile([P, N], F32, name="p_psum_%d" % c) for c in range(CHUNKS)]

        def first_product(z, c, codes, scales):
            for t in range(PACK):
                nc.tensor.matmul_mx(
                    out=a_psum[c][:, t, :],
                    lhsT=w_codes[z][:, t, :].bitcast(E5M2X4),
                    lhsT_scale=w_scale[:, t, z, :],
                    rhs=codes.bitcast(E4M3X4),
                    rhs_scale=scales,
                    start=(z == 0 and t == 0),
                    stop=(z == PASSES - 1 and t == PACK - 1),
                )

        for t in range(PACK):
            make_u_rows(0, t, 0, CHUNKS, keep.tile([P, J], F32, name="diff_0_%d" % t, align_bytes=64))
        u_early = keep.tile([P, J, PACK], BF16, name="u_early", align_bytes=64)
        nc.scalar.copy(
            u_early[:].rearrange("p (c b i) t -> p c b t i", c=CHUNKS, i=4),
            u_rows[0][:].rearrange("p c t (b i) -> p c b t i", i=4),
        )
        early_codes, early_scales = quantize(u_early, "u_early")
        w_scale = deal_w_scales()
        make_u_rows(1, 0, 0, CHUNKS, keep.tile([P, J], F32, name="diff_1_0", align_bytes=64))
        make_u_rows(1, 1, 0, CHUNKS, keep.tile([P, J], F32, name="diff_1_1", tag="w_scale_rows", align_bytes=64))
        deal_w(0, "diff_1_0")
        for c in range(CHUNKS):
            cols = slice(c * CHUNK, (c + 1) * CHUNK)
            first_product(0, c, early_codes[:, cols], early_scales[:, cols])
        late_diff = keep.tile([P, J], F32, name="late_diff", tag="u_early", align_bytes=64)
        for t in (2, 3):
            for c in range(CHUNKS):
                make_u_rows(1, t, c, 1, late_diff)
        deal_w(1, "u_early")
        u_late = [keep.tile([P, CHUNK, PACK], BF16, name="u_late_%d" % c, align_bytes=64) for c in range(CHUNKS)]
        for c in range(CHUNKS):
            nc.vector.tensor_copy(
                u_late[c][:].rearrange("p (b i) t -> p b t i", i=4),
                u_rows[1][:, c].rearrange("p t (b i) -> p b t i", i=4),
            )
        for c in range(CHUNKS):
            codes, scales = quantize(u_late[c], "u_late_%d" % c)
            first_product(1, c, codes[:], scales[:])

        hid = [keep.tile([P, CHUNK, PACK], BF16, name="hid_%d" % c, align_bytes=64) for c in range(CHUNKS)]
        for c in range(CHUNKS):
            sums = a_psum[c][:].rearrange("p t j -> p j t")
            if c == 1:
                nc.vector.tensor_scalar_max(hid[c][:], sums, 0.0)
            else:
                nc.scalar.activation(hid[c][:], sums, ACT.Relu)

        scaled_residual = keep.tile([P, CHUNKS, N], F32, name="scaled_residual", tag="w_loaded_1")
        for c in range(CHUNKS):
            nc.scalar.activation(scaled_residual[:, c, :], residual[:, c, :], ACT.Copy, scale=0.3)

        for c in range(CHUNKS):
            codes, scales = quantize(hid[c], "hid_%d" % c)
            nc.tensor.matmul_mx(
                out=p_psum[c][:],
                lhsT=codes[:].bitcast(E4M3X4),
                lhsT_scale=scales[:],
                rhs=wb_codes[:].bitcast(E5M2X4),
                rhs_scale=wb_scale[:],
                start=True,
                stop=True,
            )

        inverse = []
        for c in range(CHUNKS):
            size = keep.tile([P, N], F32, name="size_%d" % c)
            nc.scalar.activation(size[:], p_psum[c][:], ACT.Abs)
            divisor = keep.tile([P, 1], F32, name="divisor_%d" % c)
            nc.vector.tensor_scalar(size[:], size[:], 0.2, None, ALU.add, ALU.max, accum_out=divisor[:])
            inverse.append(keep.tile([P, 1], F32, name="inverse_%d" % c))
            nc.vector.reciprocal(inverse[c][:], divisor[:])
        for c in range(CHUNKS):
            result = keep.tile([P, N], F32, name="result_%d" % c)
            nc.vector.scalar_tensor_tensor(result[:], p_psum[c][:], inverse[c][:], scaled_residual[:, c, :], ALU.mult, ALU.add)
            nc.sync.dma_start(out[c * CHUNK : (c + 1) * CHUNK, :], result[:])
